import numpy as np
import ml_dtypes


def mxq(x, axis, fmt="e4m3"):
    dtype, down = {"e4m3": (ml_dtypes.float8_e4m3fn, 7), "e5m2": (ml_dtypes.float8_e5m2, 14)}[fmt]
    v = np.moveaxis(np.asarray(x, np.float32).astype(ml_dtypes.bfloat16).astype(np.float64), axis, -1)
    blocks = v.reshape(v.shape[:-1] + (-1, 32))
    amax = np.abs(blocks).max(-1, keepdims=True)
    byte = np.maximum(np.where(amax > 0, np.frexp(amax)[1] - 1 + 127, 0) - down, 1)
    scale = np.exp2(byte - 127.0)
    codes = (blocks / scale).astype(np.float32).astype(dtype).astype(np.float64)
    return np.moveaxis((codes * scale).reshape(v.shape), -1, axis)


WIDE = False


def mx_kscale(k):
    if not WIDE:
        return np.ones(k)
    levels = np.array([10, -10, 5, -5, 0])
    if k % 512:
        return np.exp2(np.random.permutation(np.resize(levels, k // 32))).repeat(32)
    a = np.empty((k // 512, 16))
    for p in range(k // 512):
        a[p, :8] = np.random.permutation(np.resize(levels, 8))
        for g in range(8):
            far = levels[np.abs(levels - a[p, g]) >= 10]
            a[p, g + 8] = far[np.random.randint(len(far))]
    return np.exp2(a.ravel()).repeat(32)


def f64(x):
    return np.asarray(x).astype(np.float64)


def striped(idx):
    return np.tile(np.asarray(idx).reshape(-1, 16).T, (8, 1)).astype(np.uint16)


def unstriped(offs):
    return offs[:16].T.reshape(-1).astype(np.int64)


B, N, T, D, DV, NQ = 1, 512, 2048, 512, 0, 384


def setup_inputs():
    n = np.random.standard_normal
    idx = np.random.permutation(T)[:B * N]
    s = mx_kscale(D)[:, None]
    return {
        "qT": (n((B, D, NQ)) * s * (1.00 / np.sqrt(D))).astype(np.float32),
        "kT": (n((D, T)) / s).astype(np.float32),
        "kb": np.tile(n(T), (128, 1)).astype(np.float32),
        "offs": striped(idx),
    }


def reference(qT, kT, kb, offs):
    idx = unstriped(offs)
    pick = lambda x: x[:, idx].reshape(x.shape[0], B, N).transpose(1, 0, 2)
    a = mxq(f64(qT), 1, "e4m3").transpose(0, 2, 1) @ mxq(pick(f64(kT)), 1, "e4m3")
    a = a + pick(f64(kb))[:, :1, :]
    out = np.zeros((B, NQ, T))
    for b in range(B):
        out[b][:, idx[b * N:(b + 1) * N]] = a[b]
    return out

@@ -1,0 +1,120 @@
+import concourse.mybir as mybir
+from concourse.masks import make_identity
+
+D, T, N, NQ = 512, 2048, 512, 384
+P = 128
+PACK = 4
+H = N // 2
+
+F32 = mybir.dt.float32
+BF16 = mybir.dt.bfloat16
+U32 = mybir.dt.uint32
+U16 = mybir.dt.uint16
+U8 = mybir.dt.uint8
+FP8X4 = mybir.dt.float8_e4m3fn_x4
+
+FLOPS = 2 * NQ * N * D
+BYTES = 4 * (D * NQ + D * T + T + NQ * T) + 2 * P * (N // 16)
+
+
+def tile_attend_sddmm_kb_kernel(tc, qT, kT, kb, offs, out):
+    nc = tc.nc
+    add = mybir.AluOpType.add
+    with (
+        tc.tile_pool(name="keep", bufs=1) as keep,
+        tc.psum_pool(name="psum", bufs=1) as psum,
+    ):
+        offsets = keep.tile([P, N // 16], U16, name="offsets")
+        nc.sync.dma_start(offsets[:], offs)
+        kb_part = keep.tile([P, T // P], F32, name="kb_part")
+        nc.scalar.dma_start(out=kb_part[:], in_=kb[0].rearrange("(p c) -> p c", c=T // P))
+
+        k_rows = kT.rearrange("(p t) n -> p t n", t=PACK)
+        planes = []
+        for t in range(PACK):
+            plane = keep.tile([P, T], F32, name=f"plane{t}")
+            nc.sync.dma_start(out=plane[:], in_=k_rows[:, t, :])
+            planes.append(plane)
+        q_rows = qT[0].rearrange("(p t) q -> p t q", t=PACK)
+        q_raw0 = keep.tile([P, PACK, P], F32, name="q_raw0")
+        nc.sync.dma_start(out=q_raw0[:], in_=q_rows[:, :, 0:P])
+        q_raw1 = keep.tile([P, PACK, NQ - P], F32, name="q_raw1")
+        nc.sync.dma_start(out=q_raw1[:], in_=q_rows[:, :, P:NQ])
+
+        ident = keep.tile([P, P], F32, name="ident")
+        make_identity(nc, ident[:])
+        windows = []
+        for m in range(3):
+            window = keep.tile([P, T], F32, name=f"window{m}")
+            nc.gpsimd.memset(window[:], 0.0)
+            windows.append(window)
+
+        kb_pool = keep.tile([P, T], F32, name="kb_pool")
+        kb_view = kb_pool[:].rearrange("q (p c) -> q p c", c=T // P)
+        for b in range(4):
+            bank = psum.tile([P, 4, P], F32, name=f"bank{b}")
+            for j in range(4):
+                c = 4 * b + j
+                nc.tensor.transpose(bank[:, j, :], kb_part[:, c : c + 1].to_broadcast([P, P]), ident[:])
+            nc.scalar.copy(out=kb_view[:, :, 4 * b : 4 * b + 4], in_=bank[:].rearrange("q c p -> q p c"))
+
+        grouped = keep.tile([P, N, PACK], BF16, name="grouped", align_bytes=64)
+        nc.vector.tensor_copy(grouped[:, :, 0], planes[0][:].indirect(offsets[:]))
+        kb_listed = keep.tile([P, N], F32, name="kb_listed")
+        nc.vector.tensor_copy(kb_listed[:], kb_pool[:].indirect(offsets[:]))
+        nc.vector.tensor_copy(grouped[:, :, 1], planes[1][:].indirect(offsets[:]))
+        nc.vector.tensor_copy(grouped[:, :, 2], planes[2][:].indirect(offsets[:]))
+        for h in range(2):
+            nc.vector.tensor_copy(
+                grouped[:, h * H : (h + 1) * H, 3],
+                planes[3][:].indirect(offsets[:, h * (H // 16) : (h + 1) * (H // 16)]),
+            )
+
+        q_grouped = keep.tile([P, NQ, PACK], BF16, name="q_grouped", align_bytes=64)
+        nc.scalar.copy(out=q_grouped[:, 0:P, :], in_=q_raw0[:].rearrange("p t q -> p q t"))
+        nc.scalar.copy(out=q_grouped[:, P:NQ, :], in_=q_raw1[:].rearrange("p t q -> p q t"))
+
+        k_codes = keep.tile([P, N], U32, name="k_codes", align_bytes=64)
+        k_scales = keep.tile([P, N], U8, name="k_scales", align_bytes=64)
+        q_codes = keep.tile([P, NQ], U32, name="q_codes", align_bytes=64)
+        q_scales = keep.tile([P, NQ], U8, name="q_scales", align_bytes=64)
+
+        def quantize(codes, scales, source, cols):
+            nc.vector.quantize_mx(
+                out=codes[:, cols].bitcast(FP8X4),
+                scales=scales[:, cols],
+                in_=source[:, cols, :].rearrange("p n t -> p (n t)"),
+            )
+
+        def multiply(acc, m, cols):
+            q_cols = slice(m * P, (m + 1) * P)
+            nc.tensor.matmul_mx(
+                out=acc,
+                lhsT=q_codes[:, q_cols].bitcast(FP8X4),
+                lhsT_scale=q_scales[:, q_cols],
+                rhs=k_codes[:, cols].bitcast(FP8X4),
+                rhs_scale=k_scales[:, cols],
+                start=True,
+                stop=True,
+            )
+
+        halves = [slice(0, H), slice(H, N)]
+        quantize(q_codes, q_scales, q_grouped, slice(0, P))
+        for cols in halves:
+            quantize(k_codes, k_scales, grouped, cols)
+        scored = keep.tile([P, N], F32, name="scored0")
+        for h, cols in enumerate(halves):
+            acc = psum.tile([P, H], F32, name=f"acc_half{h}")
+            multiply(acc[:], 0, cols)
+            nc.vector.tensor_tensor(scored[:, cols], acc[:], kb_listed[:, cols], add)
+        nc.vector.tensor_copy(windows[0][:].indirect(offsets[:]), scored[:])
+        nc.sync.dma_start(out=out[0, 0:P, :], in_=windows[0][:])
+
+        quantize(q_codes, q_scales, q_grouped, slice(P, NQ))
+        for m in range(1, 3):
+            acc = psum.tile([P, N], F32, name=f"acc{m}")
+            multiply(acc[:], m, slice(0, N))
+            scored = keep.tile([P, N], F32, name=f"scored{m}")
+            nc.vector.tensor_tensor(scored[:], acc[:], kb_listed[:], add)
+            nc.vector.tensor_copy(windows[m][:].indirect(offsets[:]), scored[:])
+            nc.sync.dma_start(out=out[0, m * P : (m + 1) * P, :], in_=windows[m][:])

@@ -24,10 +24,10 @@ def tile_attend_sddmm_kb_kernel(tc, qT, kT, kb, offs, out):
         tc.tile_pool(name="keep", bufs=1) as keep,
         tc.psum_pool(name="psum", bufs=1) as psum,
     ):
+        kb_part = keep.tile([P, T // P], F32, name="kb_part")
+        nc.sync.dma_start(out=kb_part[:], in_=kb[0].rearrange("(p c) -> p c", c=T // P))
         offsets = keep.tile([P, N // 16], U16, name="offsets")
         nc.sync.dma_start(offsets[:], offs)
-        kb_part = keep.tile([P, T // P], F32, name="kb_part")
-        nc.scalar.dma_start(out=kb_part[:], in_=kb[0].rearrange("(p c) -> p c", c=T // P))
 
         k_rows = kT.rearrange("(p t) n -> p t n", t=PACK)
         planes = []
@@ -46,8 +46,13 @@ def tile_attend_sddmm_kb_kernel(tc, qT, kT, kb, offs, out):
         windows = []
         for m in range(3):
             window = keep.tile([P, T], F32, name=f"window{m}")
-            nc.gpsimd.memset(window[:], 0.0)
             windows.append(window)
+        nc.vector.memset(windows[1][:, 0 : T // 2], 0.0)
+        nc.vector.memset(windows[2][:], 0.0)
+        nc.gpsimd.memset(windows[0][:, 0:P], 0.0)
+        nc.gpsimd.memset(windows[0][:, P : 2 * P], 0.0)
+        nc.gpsimd.memset(windows[0][:, 2 * P : T], 0.0)
+        nc.gpsimd.memset(windows[1][:, T // 2 : T], 0.0)
 
         kb_pool = keep.tile([P, T], F32, name="kb_pool")
         kb_view = kb_pool[:].rearrange("q (p c) -> q p c", c=T // P)
@@ -58,63 +63,57 @@ def tile_attend_sddmm_kb_kernel(tc, qT, kT, kb, offs, out):
                 nc.tensor.transpose(bank[:, j, :], kb_part[:, c : c + 1].to_broadcast([P, P]), ident[:])
             nc.scalar.copy(out=kb_view[:, :, 4 * b : 4 * b + 4], in_=bank[:].rearrange("q c p -> q p c"))
 
-        grouped = keep.tile([P, N, PACK], BF16, name="grouped", align_bytes=64)
-        nc.vector.tensor_copy(grouped[:, :, 0], planes[0][:].indirect(offsets[:]))
+        K0 = P
+        Q1 = P + N
+        W = N + NQ
+        grouped = keep.tile([P, W, PACK], BF16, name="grouped", align_bytes=64)
+        codes = keep.tile([P, W], U32, name="codes", align_bytes=64)
+        scales = keep.tile([P, W], U8, name="scales", align_bytes=64)
+        keys = grouped[:, K0:Q1, :]
+
         kb_listed = keep.tile([P, N], F32, name="kb_listed")
+        nc.vector.tensor_copy(keys[:, :, 0], planes[0][:].indirect(offsets[:]))
         nc.vector.tensor_copy(kb_listed[:], kb_pool[:].indirect(offsets[:]))
-        nc.vector.tensor_copy(grouped[:, :, 1], planes[1][:].indirect(offsets[:]))
-        nc.vector.tensor_copy(grouped[:, :, 2], planes[2][:].indirect(offsets[:]))
-        for h in range(2):
-            nc.vector.tensor_copy(
-                grouped[:, h * H : (h + 1) * H, 3],
-                planes[3][:].indirect(offsets[:, h * (H // 16) : (h + 1) * (H // 16)]),
+        nc.vector.tensor_copy(keys[:, 0, 1:4], kb_listed[:, 0:3])
+        for t in range(1, PACK):
+            nc.vector.tensor_copy(keys[:, :, t], planes[t][:].indirect(offsets[:]))
+
+        nc.scalar.copy(out=grouped[:, 0:K0, :], in_=q_raw0[:].rearrange("p t q -> p q t"))
+        for m in range(2):
+            nc.scalar.copy(
+                out=grouped[:, Q1 + m * P : Q1 + (m + 1) * P, :],
+                in_=q_raw1[:, :, m * P : (m + 1) * P].rearrange("p t q -> p q t"),
             )
 
-        q_grouped = keep.tile([P, NQ, PACK], BF16, name="q_grouped", align_bytes=64)
-        nc.scalar.copy(out=q_grouped[:, 0:P, :], in_=q_raw0[:].rearrange("p t q -> p q t"))
-        nc.scalar.copy(out=q_grouped[:, P:NQ, :], in_=q_raw1[:].rearrange("p t q -> p q t"))
-
-        k_codes = keep.tile([P, N], U32, name="k_codes", align_bytes=64)
-        k_scales = keep.tile([P, N], U8, name="k_scales", align_bytes=64)
-        q_codes = keep.tile([P, NQ], U32, name="q_codes", align_bytes=64)
-        q_scales = keep.tile([P, NQ], U8, name="q_scales", align_bytes=64)
-
-        def quantize(codes, scales, source, cols):
+        def quantize(start, width):
+            cols = slice(start, start + width)
             nc.vector.quantize_mx(
                 out=codes[:, cols].bitcast(FP8X4),
                 scales=scales[:, cols],
-                in_=source[:, cols, :].rearrange("p n t -> p (n t)"),
+                in_=grouped[:, cols, :].rearrange("p n t -> p (n t)"),
             )
 
-        def multiply(acc, m, cols):
-            q_cols = slice(m * P, (m + 1) * P)
+        quantize(0, 2 * P)
+        quantize(2 * P, 2 * P)
+        quantize(4 * P, P)
+        bytes_of = codes[:].bitcast(U8)
+        nc.vector.tensor_copy(bytes_of[:, 4 * Q1 : 4 * Q1 + 4], bytes_of[:, 4 * Q1 - 4 : 4 * Q1])
+        quantize(Q1, 2 * P)
+
+        for m in range(3):
+            q_start = 0 if m == 0 else Q1 + (m - 1) * P
+            q_cols = slice(q_start, q_start + P)
+            acc = psum.tile([P, N], F32, name=f"acc{m}")
             nc.tensor.matmul_mx(
-                out=acc,
-                lhsT=q_codes[:, q_cols].bitcast(FP8X4),
-                lhsT_scale=q_scales[:, q_cols],
-                rhs=k_codes[:, cols].bitcast(FP8X4),
-                rhs_scale=k_scales[:, cols],
+                out=acc[:],
+                lhsT=codes[:, q_cols].bitcast(FP8X4),
+                lhsT_scale=scales[:, q_cols],
+                rhs=codes[:, K0:Q1].bitcast(FP8X4),
+                rhs_scale=scales[:, K0:Q1],
                 start=True,
                 stop=True,
             )
-
-        halves = [slice(0, H), slice(H, N)]
-        quantize(q_codes, q_scales, q_grouped, slice(0, P))
-        for cols in halves:
-            quantize(k_codes, k_scales, grouped, cols)
-        scored = keep.tile([P, N], F32, name="scored0")
-        for h, cols in enumerate(halves):
-            acc = psum.tile([P, H], F32, name=f"acc_half{h}")
-            multiply(acc[:], 0, cols)
-            nc.vector.tensor_tensor(scored[:, cols], acc[:], kb_listed[:, cols], add)
-        nc.vector.tensor_copy(windows[0][:].indirect(offsets[:]), scored[:])
-        nc.sync.dma_start(out=out[0, 0:P, :], in_=windows[0][:])
-
-        quantize(q_codes, q_scales, q_grouped, slice(P, NQ))
-        for m in range(1, 3):
-            acc = psum.tile([P, N], F32, name=f"acc{m}")
-            multiply(acc[:], m, slice(0, N))
-            scored = keep.tile([P, N], F32, name=f"scored{m}")
-            nc.vector.tensor_tensor(scored[:], acc[:], kb_listed[:], add)
-            nc.vector.tensor_copy(windows[m][:].indirect(offsets[:]), scored[:])
+            score = keep.tile([P, N], F32, name=f"score{m}")
+            nc.vector.tensor_tensor(score[:], acc[:], kb_listed[:], add)
+            nc.vector.tensor_copy(windows[m][:].indirect(offsets[:]), score[:])
             nc.sync.dma_start(out=out[0, m * P : (m + 1) * P, :], in_=windows[m][:])

@@ -114,6 +114,11 @@ def tile_attend_sddmm_kb_kernel(tc, qT, kT, kb, offs, out):
                 stop=True,
             )
             score = keep.tile([P, N], F32, name=f"score{m}")
-            nc.vector.tensor_tensor(score[:], acc[:], kb_listed[:], add)
+            if m == 0:
+                nc.vector.tensor_tensor(score[:], acc[:], kb_listed[:], add)
+            else:
+                raw = keep.tile([P, N], F32, name=f"raw{m}")
+                nc.scalar.copy(out=raw[:], in_=acc[:])
+                nc.gpsimd.tensor_tensor(score[:], raw[:], kb_listed[:], add)
             nc.vector.tensor_copy(windows[m][:].indirect(offsets[:]), score[:])
             nc.sync.dma_start(out=out[0, m * P : (m + 1) * P, :], in_=windows[m][:])

import concourse.mybir as mybir
from concourse.masks import make_identity

D, T, N, NQ = 512, 2048, 512, 384
P = 128
PACK = 4
H = N // 2

F32 = mybir.dt.float32
BF16 = mybir.dt.bfloat16
U32 = mybir.dt.uint32
U16 = mybir.dt.uint16
U8 = mybir.dt.uint8
FP8X4 = mybir.dt.float8_e4m3fn_x4

FLOPS = 2 * NQ * N * D
BYTES = 4 * (D * NQ + D * T + T + NQ * T) + 2 * P * (N // 16)


def tile_attend_sddmm_kb_kernel(tc, qT, kT, kb, offs, out):
    nc = tc.nc
    add = mybir.AluOpType.add
    with (
        tc.tile_pool(name="keep", bufs=1) as keep,
        tc.psum_pool(name="psum", bufs=1) as psum,
    ):
        kb_part = keep.tile([P, T // P], F32, name="kb_part")
        nc.sync.dma_start(out=kb_part[:], in_=kb[0].rearrange("(p c) -> p c", c=T // P))
        offsets = keep.tile([P, N // 16], U16, name="offsets")
        nc.sync.dma_start(offsets[:], offs)

        k_rows = kT.rearrange("(p t) n -> p t n", t=PACK)
        planes = []
        for t in range(PACK):
            plane = keep.tile([P, T], F32, name=f"plane{t}")
            nc.sync.dma_start(out=plane[:], in_=k_rows[:, t, :])
            planes.append(plane)
        q_rows = qT[0].rearrange("(p t) q -> p t q", t=PACK)
        q_raw0 = keep.tile([P, PACK, P], F32, name="q_raw0")
        nc.sync.dma_start(out=q_raw0[:], in_=q_rows[:, :, 0:P])
        q_raw1 = keep.tile([P, PACK, NQ - P], F32, name="q_raw1")
        nc.sync.dma_start(out=q_raw1[:], in_=q_rows[:, :, P:NQ])

        ident = keep.tile([P, P], F32, name="ident")
        make_identity(nc, ident[:])
        windows = []
        for m in range(3):
            window = keep.tile([P, T], F32, name=f"window{m}")
            windows.append(window)
        nc.vector.memset(windows[1][:, 0 : T // 2], 0.0)
        nc.vector.memset(windows[2][:], 0.0)
        nc.gpsimd.memset(windows[0][:, 0:P], 0.0)
        nc.gpsimd.memset(windows[0][:, P : 2 * P], 0.0)
        nc.gpsimd.memset(windows[0][:, 2 * P : T], 0.0)
        nc.gpsimd.memset(windows[1][:, T // 2 : T], 0.0)

        kb_pool = keep.tile([P, T], F32, name="kb_pool")
        kb_view = kb_pool[:].rearrange("q (p c) -> q p c", c=T // P)
        for b in range(4):
            bank = psum.tile([P, 4, P], F32, name=f"bank{b}")
            for j in range(4):
                c = 4 * b + j
                nc.tensor.transpose(bank[:, j, :], kb_part[:, c : c + 1].to_broadcast([P, P]), ident[:])
            nc.scalar.copy(out=kb_view[:, :, 4 * b : 4 * b + 4], in_=bank[:].rearrange("q c p -> q p c"))

        K0 = P
        Q1 = P + N
        W = N + NQ
        grouped = keep.tile([P, W, PACK], BF16, name="grouped", align_bytes=64)
        codes = keep.tile([P, W], U32, name="codes", align_bytes=64)
        scales = keep.tile([P, W], U8, name="scales", align_bytes=64)
        keys = grouped[:, K0:Q1, :]

        kb_listed = keep.tile([P, N], F32, name="kb_listed")
        nc.vector.tensor_copy(keys[:, :, 0], planes[0][:].indirect(offsets[:]))
        nc.vector.tensor_copy(kb_listed[:], kb_pool[:].indirect(offsets[:]))
        nc.vector.tensor_copy(keys[:, 0, 1:4], kb_listed[:, 0:3])
        for t in range(1, PACK):
            nc.vector.tensor_copy(keys[:, :, t], planes[t][:].indirect(offsets[:]))

        nc.scalar.copy(out=grouped[:, 0:K0, :], in_=q_raw0[:].rearrange("p t q -> p q t"))
        for m in range(2):
            nc.scalar.copy(
                out=grouped[:, Q1 + m * P : Q1 + (m + 1) * P, :],
                in_=q_raw1[:, :, m * P : (m + 1) * P].rearrange("p t q -> p q t"),
            )

        def quantize(start, width):
            cols = slice(start, start + width)
            nc.vector.quantize_mx(
                out=codes[:, cols].bitcast(FP8X4),
                scales=scales[:, cols],
                in_=grouped[:, cols, :].rearrange("p n t -> p (n t)"),
            )

        quantize(0, 2 * P)
        quantize(2 * P, 2 * P)
        quantize(4 * P, P)
        bytes_of = codes[:].bitcast(U8)
        nc.vector.tensor_copy(bytes_of[:, 4 * Q1 : 4 * Q1 + 4], bytes_of[:, 4 * Q1 - 4 : 4 * Q1])
        quantize(Q1, 2 * P)

        for m in range(3):
            q_start = 0 if m == 0 else Q1 + (m - 1) * P
            q_cols = slice(q_start, q_start + P)
            acc = psum.tile([P, N], F32, name=f"acc{m}")
            nc.tensor.matmul_mx(
                out=acc[:],
                lhsT=codes[:, q_cols].bitcast(FP8X4),
                lhsT_scale=scales[:, q_cols],
                rhs=codes[:, K0:Q1].bitcast(FP8X4),
                rhs_scale=scales[:, K0:Q1],
                start=True,
                stop=True,
            )
            score = keep.tile([P, N], F32, name=f"score{m}")
            if m == 0:
                nc.vector.tensor_tensor(score[:], acc[:], kb_listed[:], add)
            else:
                raw = keep.tile([P, N], F32, name=f"raw{m}")
                nc.scalar.copy(out=raw[:], in_=acc[:])
                nc.gpsimd.tensor_tensor(score[:], raw[:], kb_listed[:], add)
            nc.vector.tensor_copy(windows[m][:].indirect(offsets[:]), score[:])
            nc.sync.dma_start(out=out[0, m * P : (m + 1) * P, :], in_=windows[m][:])
